import numpy as np
import ml_dtypes


def mxq(x, axis, fmt="e4m3"):
    dtype, down = {"e4m3": (ml_dtypes.float8_e4m3fn, 7), "e5m2": (ml_dtypes.float8_e5m2, 14)}[fmt]
    v = np.moveaxis(np.asarray(x, np.float32).astype(ml_dtypes.bfloat16).astype(np.float64), axis, -1)
    blocks = v.reshape(v.shape[:-1] + (-1, 32))
    amax = np.abs(blocks).max(-1, keepdims=True)
    byte = np.maximum(np.where(amax > 0, np.frexp(amax)[1] - 1 + 127, 0) - down, 1)
    scale = np.exp2(byte - 127.0)
    codes = (blocks / scale).astype(np.float32).astype(dtype).astype(np.float64)
    return np.moveaxis((codes * scale).reshape(v.shape), -1, axis)


WIDE = False


def mx_kscale(k):
    if not WIDE:
        return np.ones(k)
    levels = np.array([10, -10, 5, -5, 0])
    if k % 512:
        return np.exp2(np.random.permutation(np.resize(levels, k // 32))).repeat(32)
    a = np.empty((k // 512, 16))
    for p in range(k // 512):
        a[p, :8] = np.random.permutation(np.resize(levels, 8))
        for g in range(8):
            far = levels[np.abs(levels - a[p, g]) >= 10]
            a[p, g + 8] = far[np.random.randint(len(far))]
    return np.exp2(a.ravel()).repeat(32)


def f64(x):
    return np.asarray(x).astype(np.float64)


def striped(idx):
    return np.tile(idx.reshape(-1, 16).T, (8, 1)).astype(np.uint16)


def unstriped(offs):
    return offs[:16].T.reshape(-1).astype(np.int64)


def striped8(idx):
    return np.concatenate([x.reshape(-1, 16).T for x in idx]).astype(np.uint16)


def runs(offs, k):
    lists = np.stack([offs[16 * r : 16 * r + 16].T.reshape(-1) for r in range(8)]).astype(np.int64)
    return lists[np.arange(k) % 512 // 64]


def pack_weight(w):
    k, n = w.shape
    w = f64(np.asarray(w, np.float32).astype(ml_dtypes.bfloat16)).reshape(k // 32, 32, n)
    amax = np.abs(w).max(1)
    byte = np.clip(np.where(amax > 0, np.frexp(amax)[1] - 1 + 127 - 7, 1), 1, 254)
    scaled = (w * np.exp2(127.0 - byte)[:, None, :]).reshape(k, n).astype(np.float32)
    words = np.ascontiguousarray(scaled.reshape(k // 512, 128, 4, n).transpose(0, 1, 3, 2)).astype(ml_dtypes.float8_e4m3fn).view(np.uint8)
    return words, np.ascontiguousarray(byte.astype(np.uint8).reshape(k // 512, 16, n))


def unpack_weight(words, scales):
    g, p, n, _ = words.shape
    vals = np.ascontiguousarray(words).view(ml_dtypes.float8_e4m3fn).astype(np.float64) * np.repeat(np.exp2(scales.astype(np.float64) - 127.0), 8, axis=1)[..., None]
    return vals.transpose(0, 1, 3, 2).reshape(g * 512, n)

def planes(y):
    n, m = y.shape
    v = y.astype(np.float32).astype(ml_dtypes.bfloat16).astype(np.float64).reshape(n // 32, 32, m)
    top = np.abs(v).max(1)
    byte = np.clip(np.where(top > 0, np.frexp(top)[1] - 1 + 127 - 7, 1), 1, 254)
    codes = (v * np.exp2(127.0 - byte)[:, None, :]).reshape(n, m).astype(np.float32).astype(ml_dtypes.float8_e4m3fn).view(np.uint8)
    words = codes.reshape(n // 512, 128, 4, m).transpose(0, 1, 3, 2)
    return np.ascontiguousarray(words), np.ascontiguousarray(byte.astype(np.uint8).reshape(n // 512, 16, m))


K, T, S, H, G = 512, 1024, 256, 512, 2048


def setup_inputs():
    n = np.random.standard_normal
    s = mx_kscale(K)[:, None]
    packed_xT = pack_weight(n((K, T)) * s)
    packed_w1 = pack_weight(n((K, H)) / np.sqrt(K) / s)
    packed_w2 = pack_weight(n((K, H)) / np.sqrt(K) / s)
    packed_dT = pack_weight(n((K, G)) / s)
    return {
        "x_words": packed_xT[0],
        "x_scales": packed_xT[1],
        "w1_words": packed_w1[0],
        "w1_scales": packed_w1[1],
        "w2_words": packed_w2[0],
        "w2_scales": packed_w2[1],
        "gs": (np.random.uniform(0.5, 1.5, (K, 1)) * s).astype(np.float32),
        "d_words": packed_dT[0],
        "d_scales": packed_dT[1],
        "offs": striped(np.random.permutation(T)[:S]),
        "two": striped(np.random.permutation(T)[:S]),
        "n1": striped(np.random.permutation(S)),
        "n2": striped(np.random.permutation(S)),
        "n3": striped(np.random.permutation(S)),
        "k1": striped8(np.random.randint(0, G, (8, H))),
        "n4": striped(np.random.permutation(S)),
        "n5": striped(np.random.permutation(S)),
        "n6": striped(np.random.permutation(S)),
    }


def reference(x_words, x_scales, w1_words, w1_scales, w2_words, w2_scales, gs, d_words, d_scales, offs, two, n1, n2, n3, k1, n4, n5, n6):
    d_k1 = unpack_weight(d_words, d_scales)[np.arange(K)[:, None], runs(k1, K)]
    xq = unpack_weight(x_words, x_scales)[:, unstriped(offs)]
    y = unpack_weight(w1_words, w1_scales).T @ xq
    x_two = unpack_weight(x_words, x_scales)[:, unstriped(two)]
    d = unpack_weight(w2_words, w2_scales).T @ x_two
    z = f64(gs) * (np.maximum(np.minimum(y - (0.5 * y[:, unstriped(n1)]), d[:, unstriped(n2)]), d[:, unstriped(n3)]))
    h = 0.0625 * ((d_k1.T @ mxq(z, 0, "e4m3")))
    ex = np.exp(0.5 * h)
    out_0 = np.log((ex + ex[:, unstriped(n4)]) / (ex[:, unstriped(n5)] + ex[:, unstriped(n6)]))
    return (out_0,) + planes(out_0)

@@ -1,0 +1,182 @@
+from contextlib import ExitStack
+
+import concourse.mybir as mybir
+
+K, T, S, H, G = 512, 1024, 256, 512, 2048
+FLOPS = 3 * 2 * K * H * S
+
+F32 = mybir.dt.float32
+BF16 = mybir.dt.bfloat16
+I32 = mybir.dt.int32
+U32 = mybir.dt.uint32
+U16 = mybir.dt.uint16
+U8 = mybir.dt.uint8
+FP8X4 = mybir.dt.float8_e4m3fn_x4
+ALU = mybir.AluOpType
+ACT = mybir.ActivationFunctionType
+
+P = 128
+PACK = 4
+WIN = S + 16
+
+
+def tile_picked_twqclampbodds_none_po_kernel(tc, x_words, x_scales, w1_words, w1_scales, w2_words, w2_scales, gs, d_words, d_scales, offs, two, n1, n2, n3, k1, n4, n5, n6, out_0, out_1, out_2):
+    nc = tc.nc
+    with ExitStack() as ctx:
+        sb = ctx.enter_context(tc.tile_pool(name="sb", bufs=1))
+        ps = ctx.enter_context(tc.psum_pool(name="ps", bufs=1))
+
+        def tile(name, cols, dtype):
+            return sb.tile([P, cols], dtype, name=name, align_bytes=64)
+
+        def load_list(name, src):
+            t = sb.tile(list(src.shape), U16, name=name)
+            nc.sync.dma_start(t[:], src)
+            return t
+
+        def load_words(name, src, queue):
+            t = tile(name, src.shape[2], U32)
+            queue.dma_start(t[:].bitcast(I32), src[0].rearrange("p n t -> p (n t)").bitcast(I32))
+            return t
+
+        def zeroed(name, cols, eng):
+            t = tile(name, cols, U8)
+            eng.memset(t[:].bitcast(I32), 0)
+            return t
+
+        def load_scales(t, src, queues):
+            for q in range(4):
+                queues[q].dma_start(t[32 * q : 32 * q + 4, :].bitcast(I32), src[0, 4 * q : 4 * q + 4, :].bitcast(I32))
+
+        def deal(name, src, dtype):
+            t = tile(name, H, dtype)
+            nc.vector.tensor_copy(t[:].rearrange("p (t m) -> p m t", t=PACK), src[:].rearrange("p (m t) -> p m t", t=PACK))
+            return t
+
+        def gather(name, table, lst, n, dtype):
+            t = tile(name, n, dtype)
+            nc.vector.tensor_copy(t[:], table[:].indirect(lst[:]))
+            return t
+
+        def window(name):
+            t = tile(name, WIN, F32)
+            nc.vector.memset(t[:, S:WIN], 0.0)
+            return t
+
+        def product(bank, words, scales, t, rhs_words, rhs_scales):
+            acc = ps.tile([P, S], F32, name="acc", tag="bank%d" % bank)
+            cols = slice(P * t, P * (t + 1))
+            nc.tensor.matmul_mx(out=acc[:], lhsT=words[:, cols].bitcast(FP8X4), lhsT_scale=scales[:, cols],
+                                rhs=rhs_words[:].bitcast(FP8X4), rhs_scale=rhs_scales[:], start=True, stop=True)
+            return acc
+
+        def quantise(name, planes):
+            woven = tile(name + "_woven", PACK * S, BF16)
+            nc.vector.tensor_copy(woven[:].rearrange("p (c i t) -> p c t i", i=4, t=PACK),
+                                  planes[:].rearrange("p (t c i) -> p c t i", i=4, t=PACK))
+            words = tile(name + "_words", S, U32)
+            scales = tile(name + "_scales", S, U8)
+            nc.vector.quantize_mx(out=words[:].bitcast(FP8X4), scales=scales[:], in_=woven[:])
+            return words, scales
+
+        xs_raw = zeroed("xs_raw", T, nc.gpsimd)
+        w1s_raw = zeroed("w1s_raw", H, nc.gpsimd)
+        w2s_raw = zeroed("w2s_raw", H, nc.vector)
+        ds_raw = zeroed("ds_raw", G, nc.vector)
+        ds_plane = zeroed("ds_plane", H, nc.vector)
+        y_win = [window("y_win%d" % t) for t in range(PACK)]
+        d_win = [window("d_win%d" % t) for t in range(PACK)]
+        ex_win = [window("ex_win%d" % t) for t in range(PACK)]
+
+        offs_l = load_list("offs_l", offs)
+        xw_raw = load_words("xw_raw", x_words, nc.scalar)
+        load_scales(xs_raw, x_scales, [nc.sync] * 4)
+        w1w_raw = load_words("w1w_raw", w1_words, nc.scalar)
+        load_scales(w1s_raw, w1_scales, [nc.gpsimd, nc.gpsimd, nc.sync, nc.sync])
+        two_l = load_list("two_l", two)
+        n1_l = load_list("n1_l", n1)
+        w2w_raw = load_words("w2w_raw", w2_words, nc.sync)
+        load_scales(w2s_raw, w2_scales, [nc.sync] * 4)
+        k1_l = load_list("k1_l", k1)
+        n2_l = load_list("n2_l", n2)
+        n3_l = load_list("n3_l", n3)
+        dw_raw = load_words("dw_raw", d_words, nc.sync)
+        for b in range(2):
+            nc.gpsimd.dma_start(ds_raw[b:P:16, :].bitcast(I32), d_scales[0, b:16:2, :].bitcast(I32))
+        gain = sb.tile([P, PACK], F32, name="gain")
+        nc.gpsimd.dma_start(gain[:], gs.rearrange("(p t) o -> p (t o)", t=PACK))
+        n4_l = load_list("n4_l", n4)
+        n5_l = load_list("n5_l", n5)
+        n6_l = load_list("n6_l", n6)
+
+        xa_w = gather("xa_w", xw_raw, offs_l, S, U32)
+        xa_s = gather("xa_s", xs_raw, offs_l, S, U8)
+        w1w = deal("w1w", w1w_raw, U32)
+        w1s = deal("w1s", w1s_raw, U8)
+        y_far = []
+        for t in range(PACK):
+            acc = product(t, w1w, w1s, t, xa_w, xa_s)
+            nc.scalar.activation(y_win[t][:, 0:S], acc[:], ACT.Copy)
+            far = tile("y_far%d" % t, S, F32)
+            nc.scalar.activation(far[:], y_win[t][:].indirect(n1_l[:]), ACT.Copy)
+            y_far.append(far)
+
+        xb_w = gather("xb_w", xw_raw, two_l, S, U32)
+        xb_s = gather("xb_s", xs_raw, two_l, S, U8)
+        w2w = deal("w2w", w2w_raw, U32)
+        w2s = deal("w2s", w2s_raw, U8)
+        d_acc = [product(PACK + t, w2w, w2s, t, xb_w, xb_s) for t in range(PACK)]
+        for t in range(PACK):
+            if t < 2:
+                nc.vector.tensor_copy(d_win[t][:, 0:S], d_acc[t][:])
+            else:
+                nc.scalar.activation(d_win[t][:, 0:S], d_acc[t][:], ACT.Copy)
+
+        ds_pick = gather("ds_pick", ds_raw, k1_l, H, U8)
+        ds_dealt = deal("ds_dealt", ds_pick, U8)
+        for r in range(4):
+            src = 16 * (r // 2) + r % 2
+            nc.sync.dma_start(ds_plane[r:P:32, :].bitcast(I32), ds_dealt[src:P:32, :].bitcast(I32))
+        dw_pick = gather("dw_pick", dw_raw, k1_l, H, U32)
+        dw = deal("dw", dw_pick, U32)
+
+        z = tile("z", PACK * S, F32)
+        for t in range(PACK):
+            upper = tile("upper%d" % t, S, F32)
+            nc.scalar.activation(upper[:], d_win[t][:].indirect(n2_l[:]), ACT.Copy)
+            lower = tile("lower%d" % t, S, F32)
+            nc.scalar.activation(lower[:], d_win[t][:].indirect(n3_l[:]), ACT.Copy)
+            u = tile("u%d" % t, S, F32)
+            nc.vector.scalar_tensor_tensor(u[:], y_far[t][:], -0.5, y_win[t][:, 0:S], ALU.mult, ALU.add)
+            capped = tile("capped%d" % t, S, F32)
+            nc.vector.tensor_tensor(capped[:], u[:], upper[:], ALU.min)
+            clamped = tile("clamped%d" % t, S, F32)
+            nc.vector.tensor_tensor(clamped[:], capped[:], lower[:], ALU.max)
+            nc.vector.tensor_scalar(z[:, S * t : S * (t + 1)], clamped[:], gain[:, t : t + 1], None, ALU.mult)
+        z_words, z_scales = quantise("z", z)
+
+        for t in range(PACK):
+            acc = product(t, dw, ds_plane, t, z_words, z_scales)
+            nc.scalar.activation(ex_win[t][:, 0:S], acc[:], ACT.Exp, scale=0.5 * 0.0625)
+        sums = []
+        for t in range(PACK):
+            ex_own = tile("ex_own%d" % t, S, F32)
+            nc.vector.tensor_copy(ex_own[:], ex_win[t][:, 0:S])
+            pair = tile("pair%d" % t, 2 * S, F32)
+            nc.vector.tensor_tensor(pair[:, 0:S], ex_win[t][:].indirect(n4_l[:]), ex_own[:], ALU.add)
+            ex_far = tile("ex_far%d" % t, S, F32)
+            nc.scalar.activation(ex_far[:], ex_win[t][:].indirect(n5_l[:]), ACT.Copy)
+            nc.vector.tensor_tensor(pair[:, S : 2 * S], ex_win[t][:].indirect(n6_l[:]), ex_far[:], ALU.add)
+            sums.append(pair)
+        res = tile("res", PACK * S, F32)
+        out_rows = out_0.rearrange("(p t) j -> p t j", t=PACK)
+        for t in range(PACK):
+            logs = tile("logs%d" % t, 2 * S, F32)
+            nc.scalar.activation(logs[:], sums[t][:], ACT.Ln)
+            nc.vector.tensor_tensor(res[:, S * t : S * (t + 1)], logs[:, 0:S], logs[:, S : 2 * S], ALU.subtract)
+            nc.sync.dma_start(out_rows[:, t, :], res[:, S * t : S * (t + 1)])
+        o_words, o_scales = quantise("o", res)
+        nc.sync.dma_start(out_1[0].rearrange("p n t -> p (n t)").bitcast(I32), o_words[:].bitcast(I32))
+        for q in range(4):
+            queue = nc.scalar if q % 2 == 0 else nc.sync
+            queue.dma_start(out_2[0, 4 * q : 4 * q + 4, :].bitcast(I32), o_scales[32 * q : 32 * q + 4, :].bitcast(I32))

@@ -18,6 +18,8 @@ ACT = mybir.ActivationFunctionType
 P = 128
 PACK = 4
 WIN = S + 16
+HALF = S // 2
+HALVES = (slice(0, HALF), slice(HALF, S))
 
 
 def tile_picked_twqclampbodds_none_po_kernel(tc, x_words, x_scales, w1_words, w1_scales, w2_words, w2_scales, gs, d_words, d_scales, offs, two, n1, n2, n3, k1, n4, n5, n6, out_0, out_1, out_2):
@@ -26,8 +28,8 @@ def tile_picked_twqclampbodds_none_po_kernel(tc, x_words, x_scales, w1_words, w1
         sb = ctx.enter_context(tc.tile_pool(name="sb", bufs=1))
         ps = ctx.enter_context(tc.psum_pool(name="ps", bufs=1))
 
-        def tile(name, cols, dtype):
-            return sb.tile([P, cols], dtype, name=name, align_bytes=64)
+        def tile(name, cols, dtype, after=None):
+            return sb.tile([P, cols], dtype, name=name, tag=after or name, align_bytes=64)
 
         def load_list(name, src):
             t = sb.tile(list(src.shape), U16, name=name)
@@ -53,8 +55,8 @@ def tile_picked_twqclampbodds_none_po_kernel(tc, x_words, x_scales, w1_words, w1
             nc.vector.tensor_copy(t[:].rearrange("p (t m) -> p m t", t=PACK), src[:].rearrange("p (m t) -> p m t", t=PACK))
             return t
 
-        def gather(name, table, lst, n, dtype):
-            t = tile(name, n, dtype)
+        def gather(name, table, lst, n, dtype, after=None):
+            t = tile(name, n, dtype, after)
             nc.vector.tensor_copy(t[:], table[:].indirect(lst[:]))
             return t
 
@@ -71,15 +73,20 @@ def tile_picked_twqclampbodds_none_po_kernel(tc, x_words, x_scales, w1_words, w1
             return acc
 
         def quantise(name, planes):
-            woven = tile(name + "_woven", PACK * S, BF16)
-            nc.vector.tensor_copy(woven[:].rearrange("p (c i t) -> p c t i", i=4, t=PACK),
-                                  planes[:].rearrange("p (t c i) -> p c t i", i=4, t=PACK))
             words = tile(name + "_words", S, U32)
             scales = tile(name + "_scales", S, U8)
-            nc.vector.quantize_mx(out=words[:].bitcast(FP8X4), scales=scales[:], in_=woven[:])
+            rows = planes[:].rearrange("p (t j) -> p t j", t=PACK)
+            woven = []
+            for cols in HALVES:
+                piece = tile("%s_woven%d" % (name, cols.start), PACK * HALF, BF16)
+                nc.vector.tensor_copy(piece[:].rearrange("p (c i t) -> p c t i", i=4, t=PACK),
+                                      rows[:, :, cols].rearrange("p t (c i) -> p c t i", i=4))
+                woven.append(piece)
+            for cols, piece in zip(HALVES, woven):
+                nc.vector.quantize_mx(out=words[:, cols].bitcast(FP8X4), scales=scales[:, cols], in_=piece[:])
             return words, scales
 
-        xs_raw = zeroed("xs_raw", T, nc.gpsimd)
+        xs_raw = zeroed("xs_raw", T, nc.vector)
         w1s_raw = zeroed("w1s_raw", H, nc.gpsimd)
         w2s_raw = zeroed("w2s_raw", H, nc.vector)
         ds_raw = zeroed("ds_raw", G, nc.vector)
@@ -89,29 +96,29 @@ def tile_picked_twqclampbodds_none_po_kernel(tc, x_words, x_scales, w1_words, w1
         ex_win = [window("ex_win%d" % t) for t in range(PACK)]
 
         offs_l = load_list("offs_l", offs)
-        xw_raw = load_words("xw_raw", x_words, nc.scalar)
-        load_scales(xs_raw, x_scales, [nc.sync] * 4)
         w1w_raw = load_words("w1w_raw", w1_words, nc.scalar)
-        load_scales(w1s_raw, w1_scales, [nc.gpsimd, nc.gpsimd, nc.sync, nc.sync])
+        xw_raw = load_words("xw_raw", x_words, nc.sync)
+        load_scales(xs_raw, x_scales, [nc.sync] * 4)
+        load_scales(w1s_raw, w1_scales, [nc.sync, nc.sync, nc.sync, nc.gpsimd])
         two_l = load_list("two_l", two)
         n1_l = load_list("n1_l", n1)
         w2w_raw = load_words("w2w_raw", w2_words, nc.sync)
-        load_scales(w2s_raw, w2_scales, [nc.sync] * 4)
+        load_scales(w2s_raw, w2_scales, [nc.sync, nc.sync, nc.sync, nc.gpsimd])
         k1_l = load_list("k1_l", k1)
-        n2_l = load_list("n2_l", n2)
-        n3_l = load_list("n3_l", n3)
-        dw_raw = load_words("dw_raw", d_words, nc.sync)
         for b in range(2):
             nc.gpsimd.dma_start(ds_raw[b:P:16, :].bitcast(I32), d_scales[0, b:16:2, :].bitcast(I32))
+        dw_raw = load_words("dw_raw", d_words, nc.sync)
+        n2_l = load_list("n2_l", n2)
+        n3_l = load_list("n3_l", n3)
         gain = sb.tile([P, PACK], F32, name="gain")
-        nc.gpsimd.dma_start(gain[:], gs.rearrange("(p t) o -> p (t o)", t=PACK))
-        n4_l = load_list("n4_l", n4)
+        nc.sync.dma_start(gain[:], gs.rearrange("(p t) o -> p (t o)", t=PACK))
         n5_l = load_list("n5_l", n5)
+        n4_l = load_list("n4_l", n4)
         n6_l = load_list("n6_l", n6)
 
+        w1w = deal("w1w", w1w_raw, U32)
         xa_w = gather("xa_w", xw_raw, offs_l, S, U32)
         xa_s = gather("xa_s", xs_raw, offs_l, S, U8)
-        w1w = deal("w1w", w1w_raw, U32)
         w1s = deal("w1s", w1s_raw, U8)
         y_far = []
         for t in range(PACK):
@@ -127,12 +134,12 @@ def tile_picked_twqclampbodds_none_po_kernel(tc, x_words, x_scales, w1_words, w1
         w2s = deal("w2s", w2s_raw, U8)
         d_acc = [product(PACK + t, w2w, w2s, t, xb_w, xb_s) for t in range(PACK)]
         for t in range(PACK):
-            if t < 2:
+            if t < 1:
                 nc.vector.tensor_copy(d_win[t][:, 0:S], d_acc[t][:])
             else:
                 nc.scalar.activation(d_win[t][:, 0:S], d_acc[t][:], ACT.Copy)
 
-        ds_pick = gather("ds_pick", ds_raw, k1_l, H, U8)
+        ds_pick = gather("ds_pick", ds_raw, k1_l, H, U8, after="xb_w")
         ds_dealt = deal("ds_dealt", ds_pick, U8)
         for r in range(4):
             src = 16 * (r // 2) + r % 2
@@ -141,18 +148,24 @@ def tile_picked_twqclampbodds_none_po_kernel(tc, x_words, x_scales, w1_words, w1
         dw = deal("dw", dw_pick, U32)
 
         z = tile("z", PACK * S, F32)
+        diff = tile("diff", PACK * S, F32, after="w2s_raw")
+        capped_all = tile("capped", PACK * S, F32, after="dw_pick")
         for t in range(PACK):
             upper = tile("upper%d" % t, S, F32)
             nc.scalar.activation(upper[:], d_win[t][:].indirect(n2_l[:]), ACT.Copy)
             lower = tile("lower%d" % t, S, F32)
             nc.scalar.activation(lower[:], d_win[t][:].indirect(n3_l[:]), ACT.Copy)
-            u = tile("u%d" % t, S, F32)
-            nc.vector.scalar_tensor_tensor(u[:], y_far[t][:], -0.5, y_win[t][:, 0:S], ALU.mult, ALU.add)
-            capped = tile("capped%d" % t, S, F32)
-            nc.vector.tensor_tensor(capped[:], u[:], upper[:], ALU.min)
+            u = diff[:, S * t : S * (t + 1)]
+            nc.vector.scalar_tensor_tensor(u, y_far[t][:], -0.5, y_win[t][:, 0:S], ALU.mult, ALU.add)
+            capped = capped_all[:, S * t : S * (t + 1)]
+            nc.vector.tensor_tensor(capped, u, upper[:], ALU.min)
             clamped = tile("clamped%d" % t, S, F32)
-            nc.vector.tensor_tensor(clamped[:], capped[:], lower[:], ALU.max)
-            nc.vector.tensor_scalar(z[:, S * t : S * (t + 1)], clamped[:], gain[:, t : t + 1], None, ALU.mult)
+            z_t = z[:, S * t : S * (t + 1)]
+            pieces = HALVES if t == PACK - 1 else (slice(0, S),)
+            for cols in pieces:
+                nc.vector.tensor_tensor(clamped[:, cols], capped[:, cols], lower[:, cols], ALU.max)
+            for cols in pieces:
+                nc.vector.tensor_scalar(z_t[:, cols], clamped[:, cols], gain[:, t : t + 1], None, ALU.mult)
         z_words, z_scales = quantise("z", z)
 
         for t in range(PACK):
@@ -173,7 +186,9 @@ def tile_picked_twqclampbodds_none_po_kernel(tc, x_words, x_scales, w1_words, w1
         for t in range(PACK):
             logs = tile("logs%d" % t, 2 * S, F32)
             nc.scalar.activation(logs[:], sums[t][:], ACT.Ln)
-            nc.vector.tensor_tensor(res[:, S * t : S * (t + 1)], logs[:, 0:S], logs[:, S : 2 * S], ALU.subtract)
+            res_t = res[:, S * t : S * (t + 1)]
+            for cols in HALVES if t == PACK - 1 else (slice(0, S),):
+                nc.vector.tensor_tensor(res_t[:, cols], logs[:, 0:S][:, cols], logs[:, S : 2 * S][:, cols], ALU.subtract)
             nc.sync.dma_start(out_rows[:, t, :], res[:, S * t : S * (t + 1)])
         o_words, o_scales = quantise("o", res)
         nc.sync.dma_start(out_1[0].rearrange("p n t -> p (n t)").bitcast(I32), o_words[:].bitcast(I32))

@@ -17,59 +17,81 @@ ACT = mybir.ActivationFunctionType
 
 P = 128
 PACK = 4
-WIN = S + 16
+LAST = PACK - 1
+GROUP = 16
+QUAD = 32
+RUN = 4
+WIN = S + GROUP
+WIDE_WIN = 2 * S
 HALF = S // 2
 HALVES = (slice(0, HALF), slice(HALF, S))
 
 
-def tile_picked_twqclampbodds_none_po_kernel(tc, x_words, x_scales, w1_words, w1_scales, w2_words, w2_scales, gs, d_words, d_scales, offs, two, n1, n2, n3, k1, n4, n5, n6, out_0, out_1, out_2):
+def plane(t):
+    return slice(S * t, S * (t + 1))
+
+
+def pieces(t):
+    return HALVES if t == LAST else (slice(0, S),)
+
+
+def tile_picked_twqclampbodds_none_po_kernel(
+    tc, x_words, x_scales, w1_words, w1_scales, w2_words, w2_scales, gs, d_words, d_scales,
+    offs, two, n1, n2, n3, k1, n4, n5, n6, out_0, out_1, out_2,
+):
     nc = tc.nc
     with ExitStack() as ctx:
         sb = ctx.enter_context(tc.tile_pool(name="sb", bufs=1))
         ps = ctx.enter_context(tc.psum_pool(name="ps", bufs=1))
 
-        def tile(name, cols, dtype, after=None):
-            return sb.tile([P, cols], dtype, name=name, tag=after or name, align_bytes=64)
+        def tile(name, cols, dtype, reuses=None):
+            return sb.tile([P, cols], dtype, name=name, tag=reuses or name, align_bytes=64)
 
         def load_list(name, src):
-            t = sb.tile(list(src.shape), U16, name=name)
-            nc.sync.dma_start(t[:], src)
-            return t
+            offsets = sb.tile(list(src.shape), U16, name=name)
+            nc.sync.dma_start(offsets[:], src)
+            return offsets
 
         def load_words(name, src, queue):
-            t = tile(name, src.shape[2], U32)
-            queue.dma_start(t[:].bitcast(I32), src[0].rearrange("p n t -> p (n t)").bitcast(I32))
-            return t
+            words = tile(name, src.shape[2], U32)
+            queue.dma_start(words[:].bitcast(I32), src[0].rearrange("p n t -> p (n t)").bitcast(I32))
+            return words
 
-        def zeroed(name, cols, eng):
-            t = tile(name, cols, U8)
-            eng.memset(t[:].bitcast(I32), 0)
-            return t
+        def zeroed(name, cols, engine):
+            scales = tile(name, cols, U8)
+            engine.memset(scales[:].bitcast(I32), 0)
+            return scales
 
-        def load_scales(t, src, queues):
+        def load_scales(scales, src, queues):
             for q in range(4):
-                queues[q].dma_start(t[32 * q : 32 * q + 4, :].bitcast(I32), src[0, 4 * q : 4 * q + 4, :].bitcast(I32))
+                queues[q].dma_start(
+                    scales[QUAD * q : QUAD * q + 4, :].bitcast(I32), src[0, 4 * q : 4 * q + 4, :].bitcast(I32)
+                )
 
         def deal(name, src, dtype):
-            t = tile(name, H, dtype)
-            nc.vector.tensor_copy(t[:].rearrange("p (t m) -> p m t", t=PACK), src[:].rearrange("p (m t) -> p m t", t=PACK))
-            return t
+            dealt = tile(name, H, dtype)
+            nc.vector.tensor_copy(
+                dealt[:].rearrange("p (t m) -> p m t", t=PACK), src[:].rearrange("p (m t) -> p m t", t=PACK)
+            )
+            return dealt
 
-        def gather(name, table, lst, n, dtype, after=None):
-            t = tile(name, n, dtype, after)
-            nc.vector.tensor_copy(t[:], table[:].indirect(lst[:]))
-            return t
+        def gather(name, table, offsets, entries, dtype):
+            picked = tile(name, entries, dtype)
+            nc.vector.tensor_copy(picked[:], table[:].indirect(offsets[:]))
+            return picked
 
-        def window(name):
-            t = tile(name, WIN, F32)
-            nc.vector.memset(t[:, S:WIN], 0.0)
-            return t
+        def window(name, width=WIN):
+            win = tile(name, width, F32)
+            nc.vector.memset(win[:, S:width], 0.0)
+            return win
 
         def product(bank, words, scales, t, rhs_words, rhs_scales):
             acc = ps.tile([P, S], F32, name="acc", tag="bank%d" % bank)
             cols = slice(P * t, P * (t + 1))
-            nc.tensor.matmul_mx(out=acc[:], lhsT=words[:, cols].bitcast(FP8X4), lhsT_scale=scales[:, cols],
-                                rhs=rhs_words[:].bitcast(FP8X4), rhs_scale=rhs_scales[:], start=True, stop=True)
+            nc.tensor.matmul_mx(
+                out=acc[:], lhsT=words[:, cols].bitcast(FP8X4), lhsT_scale=scales[:, cols],
+                rhs=rhs_words[:].bitcast(FP8X4), rhs_scale=rhs_scales[:], start=True, stop=True,
+            )
             return acc
 
         def quantise(name, planes):
@@ -79,8 +101,10 @@ def tile_picked_twqclampbodds_none_po_kernel(tc, x_words, x_scales, w1_words, w1
             woven = []
             for cols in HALVES:
                 piece = tile("%s_woven%d" % (name, cols.start), PACK * HALF, BF16)
-                nc.vector.tensor_copy(piece[:].rearrange("p (c i t) -> p c t i", i=4, t=PACK),
-                                      rows[:, :, cols].rearrange("p t (c i) -> p c t i", i=4))
+                nc.vector.tensor_copy(
+                    piece[:].rearrange("p (c i t) -> p c t i", i=RUN, t=PACK),
+                    rows[:, :, cols].rearrange("p t (c i) -> p c t i", i=RUN),
+                )
                 woven.append(piece)
             for cols, piece in zip(HALVES, woven):
                 nc.vector.quantize_mx(out=words[:, cols].bitcast(FP8X4), scales=scales[:, cols], in_=piece[:])
@@ -92,7 +116,7 @@ def tile_picked_twqclampbodds_none_po_kernel(tc, x_words, x_scales, w1_words, w1
         ds_raw = zeroed("ds_raw", G, nc.vector)
         ds_plane = zeroed("ds_plane", H, nc.vector)
         y_win = [window("y_win%d" % t) for t in range(PACK)]
-        d_win = [window("d_win%d" % t) for t in range(PACK)]
+        d_win = [window("d_win%d" % t, WIDE_WIN if t == LAST else WIN) for t in range(PACK)]
         ex_win = [window("ex_win%d" % t) for t in range(PACK)]
 
         offs_l = load_list("offs_l", offs)
@@ -106,7 +130,7 @@ def tile_picked_twqclampbodds_none_po_kernel(tc, x_words, x_scales, w1_words, w1
         load_scales(w2s_raw, w2_scales, [nc.sync, nc.sync, nc.sync, nc.gpsimd])
         k1_l = load_list("k1_l", k1)
         for b in range(2):
-            nc.gpsimd.dma_start(ds_raw[b:P:16, :].bitcast(I32), d_scales[0, b:16:2, :].bitcast(I32))
+            nc.sync.dma_start(ds_raw[b:P:GROUP, :].bitcast(I32), d_scales[0, b:16:2, :].bitcast(I32))
         dw_raw = load_words("dw_raw", d_words, nc.sync)
         n2_l = load_list("n2_l", n2)
         n3_l = load_list("n3_l", n3)
@@ -133,44 +157,45 @@ def tile_picked_twqclampbodds_none_po_kernel(tc, x_words, x_scales, w1_words, w1
         w2w = deal("w2w", w2w_raw, U32)
         w2s = deal("w2s", w2s_raw, U8)
         d_acc = [product(PACK + t, w2w, w2s, t, xb_w, xb_s) for t in range(PACK)]
-        for t in range(PACK):
-            if t < 1:
-                nc.vector.tensor_copy(d_win[t][:, 0:S], d_acc[t][:])
-            else:
-                nc.scalar.activation(d_win[t][:, 0:S], d_acc[t][:], ACT.Copy)
 
-        ds_pick = gather("ds_pick", ds_raw, k1_l, H, U8, after="xb_w")
+        ds_pick = gather("ds_pick", ds_raw, k1_l, H, U8)
         ds_dealt = deal("ds_dealt", ds_pick, U8)
         for r in range(4):
-            src = 16 * (r // 2) + r % 2
-            nc.sync.dma_start(ds_plane[r:P:32, :].bitcast(I32), ds_dealt[src:P:32, :].bitcast(I32))
+            src = GROUP * (r // 2) + r % 2
+            nc.sync.dma_start(ds_plane[r:P:QUAD, :].bitcast(I32), ds_dealt[src:P:QUAD, :].bitcast(I32))
         dw_pick = gather("dw_pick", dw_raw, k1_l, H, U32)
         dw = deal("dw", dw_pick, U32)
 
         z = tile("z", PACK * S, F32)
-        diff = tile("diff", PACK * S, F32, after="w2s_raw")
-        capped_all = tile("capped", PACK * S, F32, after="dw_pick")
+        diff = tile("diff", PACK * S, F32, reuses="ds_pick")
+        capped = tile("capped", PACK * S, F32, reuses="dw_pick")
+        for t in range(PACK):
+            nc.vector.scalar_tensor_tensor(diff[:, plane(t)], y_far[t][:], -0.5, y_win[t][:, 0:S], ALU.mult, ALU.add)
+        for t in range(PACK):
+            nc.scalar.activation(d_win[t][:, 0:S], d_acc[t][:], ACT.Copy)
         for t in range(PACK):
             upper = tile("upper%d" % t, S, F32)
-            nc.scalar.activation(upper[:], d_win[t][:].indirect(n2_l[:]), ACT.Copy)
+            if t == LAST:
+                nc.vector.tensor_copy(upper[:], d_win[t][:].indirect(n2_l[:]))
+            else:
+                nc.scalar.activation(upper[:], d_win[t][:].indirect(n2_l[:]), ACT.Copy)
+            nc.vector.tensor_tensor(capped[:, plane(t)], diff[:, plane(t)], upper[:], ALU.min)
+        for t in range(PACK):
             lower = tile("lower%d" % t, S, F32)
-            nc.scalar.activation(lower[:], d_win[t][:].indirect(n3_l[:]), ACT.Copy)
-            u = diff[:, S * t : S * (t + 1)]
-            nc.vector.scalar_tensor_tensor(u, y_far[t][:], -0.5, y_win[t][:, 0:S], ALU.mult, ALU.add)
-            capped = capped_all[:, S * t : S * (t + 1)]
-            nc.vector.tensor_tensor(capped, u, upper[:], ALU.min)
             clamped = tile("clamped%d" % t, S, F32)
-            z_t = z[:, S * t : S * (t + 1)]
-            pieces = HALVES if t == PACK - 1 else (slice(0, S),)
-            for cols in pieces:
-                nc.vector.tensor_tensor(clamped[:, cols], capped[:, cols], lower[:, cols], ALU.max)
-            for cols in pieces:
-                nc.vector.tensor_scalar(z_t[:, cols], clamped[:, cols], gain[:, t : t + 1], None, ALU.mult)
+            for cols in pieces(t):
+                entries = n3_l[:, cols.start // GROUP : cols.stop // GROUP]
+                nc.scalar.activation(lower[:, cols], d_win[t][:].indirect(entries), ACT.Copy)
+            for cols in pieces(t):
+                nc.vector.tensor_tensor(clamped[:, cols], capped[:, plane(t)][:, cols], lower[:, cols], ALU.max)
+            for cols in pieces(t):
+                nc.vector.tensor_scalar(z[:, plane(t)][:, cols], clamped[:, cols], gain[:, t : t + 1], None, ALU.mult)
         z_words, z_scales = quantise("z", z)
 
         for t in range(PACK):
             acc = product(t, dw, ds_plane, t, z_words, z_scales)
             nc.scalar.activation(ex_win[t][:, 0:S], acc[:], ACT.Exp, scale=0.5 * 0.0625)
+
         sums = []
         for t in range(PACK):
             ex_own = tile("ex_own%d" % t, S, F32)
@@ -181,17 +206,22 @@ def tile_picked_twqclampbodds_none_po_kernel(tc, x_words, x_scales, w1_words, w1
             nc.scalar.activation(ex_far[:], ex_win[t][:].indirect(n5_l[:]), ACT.Copy)
             nc.vector.tensor_tensor(pair[:, S : 2 * S], ex_win[t][:].indirect(n6_l[:]), ex_far[:], ALU.add)
             sums.append(pair)
+
         res = tile("res", PACK * S, F32)
         out_rows = out_0.rearrange("(p t) j -> p t j", t=PACK)
         for t in range(PACK):
             logs = tile("logs%d" % t, 2 * S, F32)
-            nc.scalar.activation(logs[:], sums[t][:], ACT.Ln)
-            res_t = res[:, S * t : S * (t + 1)]
-            for cols in HALVES if t == PACK - 1 else (slice(0, S),):
-                nc.vector.tensor_tensor(res_t[:, cols], logs[:, 0:S][:, cols], logs[:, S : 2 * S][:, cols], ALU.subtract)
-            nc.sync.dma_start(out_rows[:, t, :], res[:, S * t : S * (t + 1)])
+            log_pair = logs[:].rearrange("p (s j) -> p s j", s=2)
+            sum_pair = sums[t][:].rearrange("p (s j) -> p s j", s=2)
+            for cols in pieces(t):
+                nc.scalar.activation(log_pair[:, :, cols], sum_pair[:, :, cols], ACT.Ln)
+                nc.vector.tensor_tensor(res[:, plane(t)][:, cols], log_pair[:, 0, cols], log_pair[:, 1, cols], ALU.subtract)
+            nc.sync.dma_start(out_rows[:, t, :], res[:, plane(t)])
+
         o_words, o_scales = quantise("o", res)
         nc.sync.dma_start(out_1[0].rearrange("p n t -> p (n t)").bitcast(I32), o_words[:].bitcast(I32))
         for q in range(4):
             queue = nc.scalar if q % 2 == 0 else nc.sync
-            queue.dma_start(out_2[0, 4 * q : 4 * q + 4, :].bitcast(I32), o_scales[32 * q : 32 * q + 4, :].bitcast(I32))
+            queue.dma_start(
+                out_2[0, 4 * q : 4 * q + 4, :].bitcast(I32), o_scales[QUAD * q : QUAD * q + 4, :].bitcast(I32)
+            )

from contextlib import ExitStack

import concourse.mybir as mybir

K, T, S, H, G = 512, 1024, 256, 512, 2048
FLOPS = 3 * 2 * K * H * S

F32 = mybir.dt.float32
BF16 = mybir.dt.bfloat16
I32 = mybir.dt.int32
U32 = mybir.dt.uint32
U16 = mybir.dt.uint16
U8 = mybir.dt.uint8
FP8X4 = mybir.dt.float8_e4m3fn_x4
ALU = mybir.AluOpType
ACT = mybir.ActivationFunctionType

P = 128
PACK = 4
LAST = PACK - 1
GROUP = 16
QUAD = 32
RUN = 4
WIN = S + GROUP
WIDE_WIN = 2 * S
HALF = S // 2
HALVES = (slice(0, HALF), slice(HALF, S))


def plane(t):
    return slice(S * t, S * (t + 1))


def pieces(t):
    return HALVES if t == LAST else (slice(0, S),)


def tile_picked_twqclampbodds_none_po_kernel(
    tc, x_words, x_scales, w1_words, w1_scales, w2_words, w2_scales, gs, d_words, d_scales,
    offs, two, n1, n2, n3, k1, n4, n5, n6, out_0, out_1, out_2,
):
    nc = tc.nc
    with ExitStack() as ctx:
        sb = ctx.enter_context(tc.tile_pool(name="sb", bufs=1))
        ps = ctx.enter_context(tc.psum_pool(name="ps", bufs=1))

        def tile(name, cols, dtype, reuses=None):
            return sb.tile([P, cols], dtype, name=name, tag=reuses or name, align_bytes=64)

        def load_list(name, src):
            offsets = sb.tile(list(src.shape), U16, name=name)
            nc.sync.dma_start(offsets[:], src)
            return offsets

        def load_words(name, src, queue):
            words = tile(name, src.shape[2], U32)
            queue.dma_start(words[:].bitcast(I32), src[0].rearrange("p n t -> p (n t)").bitcast(I32))
            return words

        def zeroed(name, cols, engine):
            scales = tile(name, cols, U8)
            engine.memset(scales[:].bitcast(I32), 0)
            return scales

        def load_scales(scales, src, queues):
            for q in range(4):
                queues[q].dma_start(
                    scales[QUAD * q : QUAD * q + 4, :].bitcast(I32), src[0, 4 * q : 4 * q + 4, :].bitcast(I32)
                )

        def deal(name, src, dtype):
            dealt = tile(name, H, dtype)
            nc.vector.tensor_copy(
                dealt[:].rearrange("p (t m) -> p m t", t=PACK), src[:].rearrange("p (m t) -> p m t", t=PACK)
            )
            return dealt

        def gather(name, table, offsets, entries, dtype):
            picked = tile(name, entries, dtype)
            nc.vector.tensor_copy(picked[:], table[:].indirect(offsets[:]))
            return picked

        def window(name, width=WIN):
            win = tile(name, width, F32)
            nc.vector.memset(win[:, S:width], 0.0)
            return win

        def product(bank, words, scales, t, rhs_words, rhs_scales):
            acc = ps.tile([P, S], F32, name="acc", tag="bank%d" % bank)
            cols = slice(P * t, P * (t + 1))
            nc.tensor.matmul_mx(
                out=acc[:], lhsT=words[:, cols].bitcast(FP8X4), lhsT_scale=scales[:, cols],
                rhs=rhs_words[:].bitcast(FP8X4), rhs_scale=rhs_scales[:], start=True, stop=True,
            )
            return acc

        def quantise(name, planes):
            words = tile(name + "_words", S, U32)
            scales = tile(name + "_scales", S, U8)
            rows = planes[:].rearrange("p (t j) -> p t j", t=PACK)
            woven = []
            for cols in HALVES:
                piece = tile("%s_woven%d" % (name, cols.start), PACK * HALF, BF16)
                nc.vector.tensor_copy(
                    piece[:].rearrange("p (c i t) -> p c t i", i=RUN, t=PACK),
                    rows[:, :, cols].rearrange("p t (c i) -> p c t i", i=RUN),
                )
                woven.append(piece)
            for cols, piece in zip(HALVES, woven):
                nc.vector.quantize_mx(out=words[:, cols].bitcast(FP8X4), scales=scales[:, cols], in_=piece[:])
            return words, scales

        xs_raw = zeroed("xs_raw", T, nc.vector)
        w1s_raw = zeroed("w1s_raw", H, nc.gpsimd)
        w2s_raw = zeroed("w2s_raw", H, nc.vector)
        ds_raw = zeroed("ds_raw", G, nc.vector)
        ds_plane = zeroed("ds_plane", H, nc.vector)
        y_win = [window("y_win%d" % t) for t in range(PACK)]
        d_win = [window("d_win%d" % t, WIDE_WIN if t == LAST else WIN) for t in range(PACK)]
        ex_win = [window("ex_win%d" % t) for t in range(PACK)]

        offs_l = load_list("offs_l", offs)
        w1w_raw = load_words("w1w_raw", w1_words, nc.scalar)
        xw_raw = load_words("xw_raw", x_words, nc.sync)
        load_scales(xs_raw, x_scales, [nc.sync] * 4)
        load_scales(w1s_raw, w1_scales, [nc.sync, nc.sync, nc.sync, nc.gpsimd])
        two_l = load_list("two_l", two)
        n1_l = load_list("n1_l", n1)
        w2w_raw = load_words("w2w_raw", w2_words, nc.sync)
        load_scales(w2s_raw, w2_scales, [nc.sync, nc.sync, nc.sync, nc.gpsimd])
        k1_l = load_list("k1_l", k1)
        for b in range(2):
            nc.sync.dma_start(ds_raw[b:P:GROUP, :].bitcast(I32), d_scales[0, b:16:2, :].bitcast(I32))
        dw_raw = load_words("dw_raw", d_words, nc.sync)
        n2_l = load_list("n2_l", n2)
        n3_l = load_list("n3_l", n3)
        gain = sb.tile([P, PACK], F32, name="gain")
        nc.sync.dma_start(gain[:], gs.rearrange("(p t) o -> p (t o)", t=PACK))
        n5_l = load_list("n5_l", n5)
        n4_l = load_list("n4_l", n4)
        n6_l = load_list("n6_l", n6)

        w1w = deal("w1w", w1w_raw, U32)
        xa_w = gather("xa_w", xw_raw, offs_l, S, U32)
        xa_s = gather("xa_s", xs_raw, offs_l, S, U8)
        w1s = deal("w1s", w1s_raw, U8)
        y_far = []
        for t in range(PACK):
            acc = product(t, w1w, w1s, t, xa_w, xa_s)
            nc.scalar.activation(y_win[t][:, 0:S], acc[:], ACT.Copy)
            far = tile("y_far%d" % t, S, F32)
            nc.scalar.activation(far[:], y_win[t][:].indirect(n1_l[:]), ACT.Copy)
            y_far.append(far)

        xb_w = gather("xb_w", xw_raw, two_l, S, U32)
        xb_s = gather("xb_s", xs_raw, two_l, S, U8)
        w2w = deal("w2w", w2w_raw, U32)
        w2s = deal("w2s", w2s_raw, U8)
        d_acc = [product(PACK + t, w2w, w2s, t, xb_w, xb_s) for t in range(PACK)]

        ds_pick = gather("ds_pick", ds_raw, k1_l, H, U8)
        ds_dealt = deal("ds_dealt", ds_pick, U8)
        for r in range(4):
            src = GROUP * (r // 2) + r % 2
            nc.sync.dma_start(ds_plane[r:P:QUAD, :].bitcast(I32), ds_dealt[src:P:QUAD, :].bitcast(I32))
        dw_pick = gather("dw_pick", dw_raw, k1_l, H, U32)
        dw = deal("dw", dw_pick, U32)

        z = tile("z", PACK * S, F32)
        diff = tile("diff", PACK * S, F32, reuses="ds_pick")
        capped = tile("capped", PACK * S, F32, reuses="dw_pick")
        for t in range(PACK):
            nc.vector.scalar_tensor_tensor(diff[:, plane(t)], y_far[t][:], -0.5, y_win[t][:, 0:S], ALU.mult, ALU.add)
        for t in range(PACK):
            nc.scalar.activation(d_win[t][:, 0:S], d_acc[t][:], ACT.Copy)
        for t in range(PACK):
            upper = tile("upper%d" % t, S, F32)
            if t == LAST:
                nc.vector.tensor_copy(upper[:], d_win[t][:].indirect(n2_l[:]))
            else:
                nc.scalar.activation(upper[:], d_win[t][:].indirect(n2_l[:]), ACT.Copy)
            nc.vector.tensor_tensor(capped[:, plane(t)], diff[:, plane(t)], upper[:], ALU.min)
        for t in range(PACK):
            lower = tile("lower%d" % t, S, F32)
            clamped = tile("clamped%d" % t, S, F32)
            for cols in pieces(t):
                entries = n3_l[:, cols.start // GROUP : cols.stop // GROUP]
                nc.scalar.activation(lower[:, cols], d_win[t][:].indirect(entries), ACT.Copy)
            for cols in pieces(t):
                nc.vector.tensor_tensor(clamped[:, cols], capped[:, plane(t)][:, cols], lower[:, cols], ALU.max)
            for cols in pieces(t):
                nc.vector.tensor_scalar(z[:, plane(t)][:, cols], clamped[:, cols], gain[:, t : t + 1], None, ALU.mult)
        z_words, z_scales = quantise("z", z)

        for t in range(PACK):
            acc = product(t, dw, ds_plane, t, z_words, z_scales)
            nc.scalar.activation(ex_win[t][:, 0:S], acc[:], ACT.Exp, scale=0.5 * 0.0625)

        sums = []
        for t in range(PACK):
            ex_own = tile("ex_own%d" % t, S, F32)
            nc.vector.tensor_copy(ex_own[:], ex_win[t][:, 0:S])
            pair = tile("pair%d" % t, 2 * S, F32)
            nc.vector.tensor_tensor(pair[:, 0:S], ex_win[t][:].indirect(n4_l[:]), ex_own[:], ALU.add)
            ex_far = tile("ex_far%d" % t, S, F32)
            nc.scalar.activation(ex_far[:], ex_win[t][:].indirect(n5_l[:]), ACT.Copy)
            nc.vector.tensor_tensor(pair[:, S : 2 * S], ex_win[t][:].indirect(n6_l[:]), ex_far[:], ALU.add)
            sums.append(pair)

        res = tile("res", PACK * S, F32)
        out_rows = out_0.rearrange("(p t) j -> p t j", t=PACK)
        for t in range(PACK):
            logs = tile("logs%d" % t, 2 * S, F32)
            log_pair = logs[:].rearrange("p (s j) -> p s j", s=2)
            sum_pair = sums[t][:].rearrange("p (s j) -> p s j", s=2)
            for cols in pieces(t):
                nc.scalar.activation(log_pair[:, :, cols], sum_pair[:, :, cols], ACT.Ln)
                nc.vector.tensor_tensor(res[:, plane(t)][:, cols], log_pair[:, 0, cols], log_pair[:, 1, cols], ALU.subtract)
            nc.sync.dma_start(out_rows[:, t, :], res[:, plane(t)])

        o_words, o_scales = quantise("o", res)
        nc.sync.dma_start(out_1[0].rearrange("p n t -> p (n t)").bitcast(I32), o_words[:].bitcast(I32))
        for q in range(4):
            queue = nc.scalar if q % 2 == 0 else nc.sync
            queue.dma_start(
                out_2[0, 4 * q : 4 * q + 4, :].bitcast(I32), o_scales[QUAD * q : QUAD * q + 4, :].bitcast(I32)
            )
